import numpy as np, ml_dtypes
CORES = [19,147,275,403]
N = 4
GR, GC = 2, 2
L, KA, KB, F = 4, 2, 2, 256
def setup_inputs(rng):
    return {"a": rng.standard_normal((N, 128, KA * 128), dtype=np.float32).astype(ml_dtypes.bfloat16), "b": rng.standard_normal((N, 128, KB * F), dtype=np.float32).astype(ml_dtypes.bfloat16)}
def setup_inputs_big(rng):
    d = setup_inputs(rng)
    for k in ("a", "b"): d[k] = (d[k].astype(np.float32) * 1024.0).astype(d[k].dtype)
    return d
def setup_inputs_small(rng):
    d = setup_inputs(rng)
    for k in ("a", "b"): d[k] = (d[k].astype(np.float32) * (1 / 1024.0)).astype(d[k].dtype)
    return d
def setup_inputs_apart(rng):
    d = setup_inputs(rng)
    f = (10.0 ** rng.permutation(np.linspace(-1.5, 1.5, N))).astype(np.float32).reshape(N, 1, 1)
    for k in ("a", "b"): d[k] = (d[k].astype(np.float32) * f).astype(d[k].dtype)
    return d
def reference(a, b):
    A, B = a.astype(np.float64), b.astype(np.float64)
    y = np.zeros((N, 128, F))
    for i in range(GR):
        for j in range(GC):
            for k in range(L):
                At = A[i * GC + k // KA][:, 128 * (k % KA):128 * (k % KA) + 128]
                Bt = B[(k // KB) * GC + j][:, F * (k % KB):F * (k % KB) + F]
                y[i * GC + j] += At.T @ Bt
    return {"y": y.astype(ml_dtypes.bfloat16 if a.dtype != np.float64 else np.float64)}

@@ -1,0 +1,95 @@
+GR, GC = 2, 2
+L, KA, KB, F = 4, 2, 2, 256
+M = 128
+
+SCRATCH = {
+    "b_stage": ("dram", [128, KB * F], "bfloat16"),
+    "b_hop": ("dram", [128, KB * F], "bfloat16"),
+    "a_own": ("sbuf", [128, KA * M], "bfloat16"),
+    "b_own": ("sbuf", [128, KB * F], "bfloat16"),
+    "a_row": ("sbuf", [128, KA * M], "bfloat16"),
+    "b_col": ("sbuf", [128, KB * F], "bfloat16"),
+    "y_out": ("sbuf", [128, F], "bfloat16"),
+    "acc": ("psum", [128, F], "float32"),
+}
+SEMAPHORES = ["staged", "a_in", "b_in", "a_got", "hop_got", "col_got", "sent", "mm_done", "cast_done", "stored"]
+
+
+def _engines(mask):
+    return bin(mask).count("1")
+
+
+def _col_peer(cores, r):
+    return cores[(1 - r // GC) * GC + r % GC]
+
+
+def _via(topo, cores, src, dst):
+    ways = [m for m in cores if m != src and m != dst and topo.may_write(src, m) and topo.may_write(m, dst)]
+    far = [m for m in ways if topo.rack(topo.host(m)) != topo.rack(topo.host(src))]
+    return (far + ways)[0]
+
+
+def rank_program(g, core, T, topo):
+    rank = T.rank_of(core)
+    if rank is None:
+        return
+    S, cores = T.sem, T.cores
+    row, col = rank // GC, rank % GC
+    row_peer = cores[row * GC + (1 - col)]
+    middle = _via(topo, cores, core, _col_peer(cores, rank))
+    feeder = [r for r in range(len(cores))
+              if cores[r] != core and _via(topo, cores, cores[r], _col_peer(cores, r)) == core][0]
+    onward = _col_peer(cores, feeder)
+    bringer = _via(topo, cores, _col_peer(cores, rank), core)
+    sent = [0]
+
+    def send(out_ap, in_ap, dst, sem):
+        rid, pid = topo.addr(dst, core)
+        mask = topo.mask(core, dst)
+        g.remote_dma(out_ap=out_ap, in_ap=in_ap, remote_sem=sem, local_sem=S.sent,
+                     pid=pid, routing_id=rid, dma_engine_mask=mask)
+        sent[0] += _engines(mask)
+
+    g.sync.dma_start(T.b_stage[:], T.b[:]).then_inc(S.staged, 16)
+    g.scalar.wait_ge(S.staged, 16)
+    g.scalar.dma_start(T.a_own[:], T.a[:]).then_inc(S.a_in, 16)
+    g.scalar.dma_start(T.b_own[:], T.b[:]).then_inc(S.b_in, 16)
+
+    g.wait_ge(S.staged, 16)
+    send(T.b_hop[:], T.b_stage[:], middle, S.hop_got)
+    g.wait_ge(S.a_in, 16)
+    send(T.a_row[:], T.a_own[:], row_peer, S.a_got)
+    g.wait_ge(S.hop_got, _engines(topo.mask(cores[feeder], core)))
+    send(T.b_col[:], T.b_hop[:], onward, S.col_got)
+
+    te = g.tensor
+    terms = sorted((k // KB != row, k // KA != col, k) for k in range(L))
+    waited = set()
+
+    def need(name, val):
+        if name not in waited:
+            te.wait_ge(S[name], val)
+            waited.add(name)
+
+    for n, (b_far, a_far, k) in enumerate(terms):
+        ta, tb = k % KA, k % KB
+        if a_far:
+            need("a_got", _engines(topo.mask(row_peer, core)))
+            lhsT = T.a_row[:, ta * M:(ta + 1) * M]
+        else:
+            need("a_in", 16)
+            lhsT = T.a_own[:, ta * M:(ta + 1) * M]
+        if b_far:
+            need("col_got", _engines(topo.mask(bringer, core)))
+            rhs = T.b_col[:, tb * F:(tb + 1) * F]
+        else:
+            need("b_in", 16)
+            rhs = T.b_own[:, tb * F:(tb + 1) * F]
+        te.matmul(T.acc[:], lhsT, rhs, start=(n == 0), stop=(n == L - 1)).then_inc(S.mm_done, 1)
+
+    g.vector.wait_ge(S.mm_done, L)
+    g.vector.tensor_copy(T.y_out[:], T.acc[:]).then_inc(S.cast_done, 1)
+    g.sync.wait_ge(S.cast_done, 1)
+    g.sync.dma_start(T.y[:], T.y_out[:]).then_inc(S.stored, 16)
+    g.sync.wait_ge(S.stored, 16)
+    g.wait_ge(S.sent, sent[0])

@@ -1,18 +1,23 @@
+from concourse.bass import DstId, RemoteDMATransfer
+
 GR, GC = 2, 2
 L, KA, KB, F = 4, 2, 2, 256
 M = 128
+H = 2
 
 SCRATCH = {
-    "b_stage": ("dram", [128, KB * F], "bfloat16"),
-    "b_hop": ("dram", [128, KB * F], "bfloat16"),
-    "a_own": ("sbuf", [128, KA * M], "bfloat16"),
-    "b_own": ("sbuf", [128, KB * F], "bfloat16"),
-    "a_row": ("sbuf", [128, KA * M], "bfloat16"),
-    "b_col": ("sbuf", [128, KB * F], "bfloat16"),
+    "b_stage": ("dram", [H, 128, F], "bfloat16"),
+    "a_stage": ("dram", [H, 128, M], "bfloat16"),
+    "b_hop": ("dram", [H, 128, F], "bfloat16"),
+    "a_own": ("sbuf", [128, H * M], "bfloat16"),
+    "b_own": ("sbuf", [128, H * F], "bfloat16"),
+    "a_row": ("sbuf", [128, H * M], "bfloat16"),
+    "b_col": ("sbuf", [128, H * F], "bfloat16"),
     "y_out": ("sbuf", [128, F], "bfloat16"),
     "acc": ("psum", [128, F], "float32"),
 }
-SEMAPHORES = ["staged", "a_in", "b_in", "a_got", "hop_got", "col_got", "sent", "mm_done", "cast_done", "stored"]
+SEMAPHORES = (["b_staged", "a_staged", "a_in", "b_in", "a_got", "sent", "mm_done", "cast_done", "stored"]
+              + ["hop_got%d" % p for p in range(H)] + ["col_got%d" % p for p in range(H)])
 
 
 def _engines(mask):
@@ -23,10 +28,19 @@ def _col_peer(cores, r):
     return cores[(1 - r // GC) * GC + r % GC]
 
 
-def _via(topo, cores, src, dst):
+def _other_rack(topo, x, y):
+    return topo.rack(topo.host(x)) != topo.rack(topo.host(y))
+
+
+def _lanes(topo, src, dst):
+    mask = topo.mask(src, dst)
+    bits = [1 << i for i in range(mask.bit_length()) if mask >> i & 1]
+    return sum(bits[1::2] if _other_rack(topo, src, dst) else bits[0::2])
+
+
+def _vias(topo, cores, src, dst):
     ways = [m for m in cores if m != src and m != dst and topo.may_write(src, m) and topo.may_write(m, dst)]
-    far = [m for m in ways if topo.rack(topo.host(m)) != topo.rack(topo.host(src))]
-    return (far + ways)[0]
+    return sorted(ways, key=lambda m: not _other_rack(topo, src, m))[:H]
 
 
 def rank_program(g, core, T, topo):
@@ -36,34 +50,55 @@ def rank_program(g, core, T, topo):
     S, cores = T.sem, T.cores
     row, col = rank // GC, rank % GC
     row_peer = cores[row * GC + (1 - col)]
-    middle = _via(topo, cores, core, _col_peer(cores, rank))
-    feeder = [r for r in range(len(cores))
-              if cores[r] != core and _via(topo, cores, cores[r], _col_peer(cores, r)) == core][0]
-    onward = _col_peer(cores, feeder)
-    bringer = _via(topo, cores, _col_peer(cores, rank), core)
+    col_peer = _col_peer(cores, rank)
+    out_via = _vias(topo, cores, core, col_peer)
+    in_via = _vias(topo, cores, col_peer, core)
+    passing = {}
+    for r in range(len(cores)):
+        if cores[r] != core:
+            for p, m in enumerate(_vias(topo, cores, cores[r], _col_peer(cores, r))):
+                if m == core:
+                    passing[p] = (cores[r], _col_peer(cores, r))
     sent = [0]
 
     def send(out_ap, in_ap, dst, sem):
         rid, pid = topo.addr(dst, core)
-        mask = topo.mask(core, dst)
+        mask = _lanes(topo, core, dst)
         g.remote_dma(out_ap=out_ap, in_ap=in_ap, remote_sem=sem, local_sem=S.sent,
                      pid=pid, routing_id=rid, dma_engine_mask=mask)
         sent[0] += _engines(mask)
 
-    g.sync.dma_start(T.b_stage[:], T.b[:]).then_inc(S.staged, 16)
-    g.scalar.wait_ge(S.staged, 16)
-    g.scalar.dma_start(T.a_own[:], T.a[:]).then_inc(S.a_in, 16)
-    g.scalar.dma_start(T.b_own[:], T.b[:]).then_inc(S.b_in, 16)
+    g.sync.dma_start(T.b_stage[:], T.b[:]).then_inc(S.b_staged, 16)
+    g.sync.dma_start(T.a_stage[:], T.a[:]).then_inc(S.a_staged, 16)
+    g.scalar.wait_ge(S.a_staged, 16)
+    for p in range(H):
+        g.scalar.dma_start(T.a_own[:, p * M:(p + 1) * M], T.a_stage[p]).then_inc(S.a_in, 16)
+    g.scalar.wait_ge(S.b_staged, 16)
+    for p in range(H):
+        g.scalar.dma_start(T.b_own[:, p * F:(p + 1) * F], T.b_stage[p]).then_inc(S.b_in, 16)
 
-    g.wait_ge(S.staged, 16)
-    send(T.b_hop[:], T.b_stage[:], middle, S.hop_got)
-    g.wait_ge(S.a_in, 16)
+    g.wait_ge(S.b_staged, 16)
+    transfers = []
+    for p, m in enumerate(out_via):
+        rid, pid = topo.addr(m, core)
+        mask = _lanes(topo, core, m)
+        transfers.append(RemoteDMATransfer(dst_ids=[DstId(rid=rid, pnc=pid)], dma_engine_mask=mask,
+                                           remote_sem=S["hop_got%d" % p], src=T.b_stage[p], dst=T.b_hop[p]))
+        sent[0] += _engines(mask)
+    g.remote_dma_fused(transfers, local_sem=S.sent)
+
+    g.wait_ge(S.a_in, 16 * H)
     send(T.a_row[:], T.a_own[:], row_peer, S.a_got)
-    g.wait_ge(S.hop_got, _engines(topo.mask(cores[feeder], core)))
-    send(T.b_col[:], T.b_hop[:], onward, S.col_got)
+
+    order = sorted(passing, key=lambda p: not _other_rack(topo, core, passing[p][1]))
+    for p in order:
+        owner, dst = passing[p]
+        g.wait_ge(S["hop_got%d" % p], _engines(_lanes(topo, owner, core)))
+        send(T.b_col[:, p * F:(p + 1) * F], T.b_hop[p], dst, S["col_got%d" % p])
 
     te = g.tensor
-    terms = sorted((k // KB != row, k // KA != col, k) for k in range(L))
+    late = sorted(range(H), key=lambda p: not _other_rack(topo, in_via[p], core))
+    terms = [(row, p) for p in range(H)] + [(1 - row, p) for p in late]
     waited = set()
 
     def need(name, val):
@@ -71,23 +106,22 @@ def rank_program(g, core, T, topo):
             te.wait_ge(S[name], val)
             waited.add(name)
 
-    for n, (b_far, a_far, k) in enumerate(terms):
-        ta, tb = k % KA, k % KB
-        if a_far:
-            need("a_got", _engines(topo.mask(row_peer, core)))
-            lhsT = T.a_row[:, ta * M:(ta + 1) * M]
+    for n, (kb, p) in enumerate(terms):
+        if kb == col:
+            need("a_in", 16 * H)
+            lhsT = T.a_own[:, p * M:(p + 1) * M]
         else:
-            need("a_in", 16)
-            lhsT = T.a_own[:, ta * M:(ta + 1) * M]
-        if b_far:
-            need("col_got", _engines(topo.mask(bringer, core)))
-            rhs = T.b_col[:, tb * F:(tb + 1) * F]
+            need("a_got", _engines(_lanes(topo, row_peer, core)))
+            lhsT = T.a_row[:, p * M:(p + 1) * M]
+        if kb == row:
+            need("b_in", 16 * H)
+            rhs = T.b_own[:, p * F:(p + 1) * F]
         else:
-            need("b_in", 16)
-            rhs = T.b_own[:, tb * F:(tb + 1) * F]
-        te.matmul(T.acc[:], lhsT, rhs, start=(n == 0), stop=(n == L - 1)).then_inc(S.mm_done, 1)
+            need("col_got%d" % p, _engines(_lanes(topo, in_via[p], core)))
+            rhs = T.b_col[:, p * F:(p + 1) * F]
+        te.matmul(T.acc[:], lhsT, rhs, start=(n == 0), stop=(n == len(terms) - 1)).then_inc(S.mm_done, 1)
 
-    g.vector.wait_ge(S.mm_done, L)
+    g.vector.wait_ge(S.mm_done, len(terms))
     g.vector.tensor_copy(T.y_out[:], T.acc[:]).then_inc(S.cast_done, 1)
     g.sync.wait_ge(S.cast_done, 1)
     g.sync.dma_start(T.y[:], T.y_out[:]).then_inc(S.stored, 16)

from concourse.bass import DstId, RemoteDMATransfer

GR, GC = 2, 2
L, KA, KB, F = 4, 2, 2, 256
M = 128
H = 2

SCRATCH = {
    "b_stage": ("dram", [H, 128, F], "bfloat16"),
    "a_stage": ("dram", [H, 128, M], "bfloat16"),
    "b_hop": ("dram", [H, 128, F], "bfloat16"),
    "a_own": ("sbuf", [128, H * M], "bfloat16"),
    "b_own": ("sbuf", [128, H * F], "bfloat16"),
    "a_row": ("sbuf", [128, H * M], "bfloat16"),
    "b_col": ("sbuf", [128, H * F], "bfloat16"),
    "y_out": ("sbuf", [128, F], "bfloat16"),
    "acc": ("psum", [128, F], "float32"),
}
SEMAPHORES = (["b_staged", "a_staged", "a_in", "b_in", "a_got", "sent", "mm_done", "cast_done", "stored"]
              + ["hop_got%d" % p for p in range(H)] + ["col_got%d" % p for p in range(H)])


def _engines(mask):
    return bin(mask).count("1")


def _col_peer(cores, r):
    return cores[(1 - r // GC) * GC + r % GC]


def _other_rack(topo, x, y):
    return topo.rack(topo.host(x)) != topo.rack(topo.host(y))


def _lanes(topo, src, dst):
    mask = topo.mask(src, dst)
    bits = [1 << i for i in range(mask.bit_length()) if mask >> i & 1]
    return sum(bits[1::2] if _other_rack(topo, src, dst) else bits[0::2])


def _vias(topo, cores, src, dst):
    ways = [m for m in cores if m != src and m != dst and topo.may_write(src, m) and topo.may_write(m, dst)]
    return sorted(ways, key=lambda m: not _other_rack(topo, src, m))[:H]


def rank_program(g, core, T, topo):
    rank = T.rank_of(core)
    if rank is None:
        return
    S, cores = T.sem, T.cores
    row, col = rank // GC, rank % GC
    row_peer = cores[row * GC + (1 - col)]
    col_peer = _col_peer(cores, rank)
    out_via = _vias(topo, cores, core, col_peer)
    in_via = _vias(topo, cores, col_peer, core)
    passing = {}
    for r in range(len(cores)):
        if cores[r] != core:
            for p, m in enumerate(_vias(topo, cores, cores[r], _col_peer(cores, r))):
                if m == core:
                    passing[p] = (cores[r], _col_peer(cores, r))
    sent = [0]

    def send(out_ap, in_ap, dst, sem):
        rid, pid = topo.addr(dst, core)
        mask = _lanes(topo, core, dst)
        g.remote_dma(out_ap=out_ap, in_ap=in_ap, remote_sem=sem, local_sem=S.sent,
                     pid=pid, routing_id=rid, dma_engine_mask=mask)
        sent[0] += _engines(mask)

    g.sync.dma_start(T.b_stage[:], T.b[:]).then_inc(S.b_staged, 16)
    g.sync.dma_start(T.a_stage[:], T.a[:]).then_inc(S.a_staged, 16)
    g.scalar.wait_ge(S.a_staged, 16)
    for p in range(H):
        g.scalar.dma_start(T.a_own[:, p * M:(p + 1) * M], T.a_stage[p]).then_inc(S.a_in, 16)
    g.scalar.wait_ge(S.b_staged, 16)
    for p in range(H):
        g.scalar.dma_start(T.b_own[:, p * F:(p + 1) * F], T.b_stage[p]).then_inc(S.b_in, 16)

    g.wait_ge(S.b_staged, 16)
    transfers = []
    for p, m in enumerate(out_via):
        rid, pid = topo.addr(m, core)
        mask = _lanes(topo, core, m)
        transfers.append(RemoteDMATransfer(dst_ids=[DstId(rid=rid, pnc=pid)], dma_engine_mask=mask,
                                           remote_sem=S["hop_got%d" % p], src=T.b_stage[p], dst=T.b_hop[p]))
        sent[0] += _engines(mask)
    g.remote_dma_fused(transfers, local_sem=S.sent)

    g.wait_ge(S.a_in, 16 * H)
    send(T.a_row[:], T.a_own[:], row_peer, S.a_got)

    order = sorted(passing, key=lambda p: not _other_rack(topo, core, passing[p][1]))
    for p in order:
        owner, dst = passing[p]
        g.wait_ge(S["hop_got%d" % p], _engines(_lanes(topo, owner, core)))
        send(T.b_col[:, p * F:(p + 1) * F], T.b_hop[p], dst, S["col_got%d" % p])

    te = g.tensor
    late = sorted(range(H), key=lambda p: not _other_rack(topo, in_via[p], core))
    terms = [(row, p) for p in range(H)] + [(1 - row, p) for p in late]
    waited = set()

    def need(name, val):
        if name not in waited:
            te.wait_ge(S[name], val)
            waited.add(name)

    for n, (kb, p) in enumerate(terms):
        if kb == col:
            need("a_in", 16 * H)
            lhsT = T.a_own[:, p * M:(p + 1) * M]
        else:
            need("a_got", _engines(_lanes(topo, row_peer, core)))
            lhsT = T.a_row[:, p * M:(p + 1) * M]
        if kb == row:
            need("b_in", 16 * H)
            rhs = T.b_own[:, p * F:(p + 1) * F]
        else:
            need("col_got%d" % p, _engines(_lanes(topo, in_via[p], core)))
            rhs = T.b_col[:, p * F:(p + 1) * F]
        te.matmul(T.acc[:], lhsT, rhs, start=(n == 0), stop=(n == len(terms) - 1)).then_inc(S.mm_done, 1)

    g.vector.wait_ge(S.mm_done, len(terms))
    g.vector.tensor_copy(T.y_out[:], T.acc[:]).then_inc(S.cast_done, 1)
    g.sync.wait_ge(S.cast_done, 1)
    g.sync.dma_start(T.y[:], T.y_out[:]).then_inc(S.stored, 16)
    g.sync.wait_ge(S.stored, 16)
    g.wait_ge(S.sent, sent[0])
